import numpy as np
import ml_dtypes


def mxq(x, axis, fmt="e4m3"):
    dtype, down = {"e4m3": (ml_dtypes.float8_e4m3fn, 7), "e5m2": (ml_dtypes.float8_e5m2, 14)}[fmt]
    v = np.moveaxis(np.asarray(x, np.float32).astype(ml_dtypes.bfloat16).astype(np.float64), axis, -1)
    blocks = v.reshape(v.shape[:-1] + (-1, 32))
    amax = np.abs(blocks).max(-1, keepdims=True)
    byte = np.maximum(np.where(amax > 0, np.frexp(amax)[1] - 1 + 127, 0) - down, 1)
    scale = np.exp2(byte - 127.0)
    codes = (blocks / scale).astype(np.float32).astype(dtype).astype(np.float64)
    return np.moveaxis((codes * scale).reshape(v.shape), -1, axis)


WIDE = False


def mx_kscale(k):
    if not WIDE:
        return np.ones(k)
    levels = np.array([10, -10, 5, -5, 0])
    if k % 512:
        return np.exp2(np.random.permutation(np.resize(levels, k // 32))).repeat(32)
    a = np.empty((k // 512, 16))
    for p in range(k // 512):
        a[p, :8] = np.random.permutation(np.resize(levels, 8))
        for g in range(8):
            far = levels[np.abs(levels - a[p, g]) >= 10]
            a[p, g + 8] = far[np.random.randint(len(far))]
    return np.exp2(a.ravel()).repeat(32)


def f64(x):
    return np.asarray(x).astype(np.float64)


def striped(idx):
    return np.tile(np.asarray(idx).reshape(-1, 16).T, (8, 1)).astype(np.uint16)


def unstriped(offs):
    return offs[:16].T.reshape(-1).astype(np.int64)


E2M1 = np.array([0.0, 0.5, 1.0, 1.5, 2.0, 3.0, 4.0, 6.0, -0.0, -0.5, -1.0, -1.5, -2.0, -3.0, -4.0, -6.0])


def pack_weight(w, fmt):
    k, n = w.shape
    w = f64(np.asarray(w, np.float32).astype(ml_dtypes.bfloat16)).reshape(k // 32, 32, n)
    amax = np.abs(w).max(1)
    if fmt == "e4m3":
        byte = np.frexp(amax)[1] - 1 + 127 - 7
    else:
        mant, ex = np.frexp(amax / 6.0)
        byte = np.where(mant > 0.5, ex, ex - 1) + 127
    byte = np.clip(np.where(amax > 0, byte, 1), 1, 254)
    scaled = (w * np.exp2(127.0 - byte)[:, None, :]).reshape(k, n).astype(np.float32)
    by_word = np.ascontiguousarray(scaled.reshape(k // 512, 128, 4, n).transpose(0, 1, 3, 2))
    if fmt == "e4m3":
        words = by_word.astype(ml_dtypes.float8_e4m3fn).view(np.uint8)
    else:
        c = by_word.astype(ml_dtypes.float4_e2m1fn).view(np.uint8) & 0xF
        words = (c[..., 0::2] | (c[..., 1::2] << 4)).reshape(k // 512, 128, 2 * n)
    return np.ascontiguousarray(words), np.ascontiguousarray(byte.astype(np.uint8).reshape(k // 512, 16, n))


def unpack_weight(words, scales, fmt):
    g, _, n = scales.shape
    words = np.ascontiguousarray(words).reshape(g, 128, n, -1)
    if fmt == "e4m3":
        vals = words.view(ml_dtypes.float8_e4m3fn).astype(np.float64)
    else:
        nib = np.empty((g, 128, n, 4), np.uint8)
        nib[..., 0::2] = words & 0xF
        nib[..., 1::2] = words >> 4
        vals = E2M1[nib]
    vals = vals * np.repeat(np.exp2(scales.astype(np.float64) - 127.0), 8, axis=1)[..., None]
    return vals.transpose(0, 1, 3, 2).reshape(g * 512, n)


K, T, J, N = 1024, 2048, 512, 512


def setup_inputs():
    n = np.random.standard_normal
    idx = np.random.permutation(T)[:J]
    fk = mx_kscale(K)
    xqp = pack_weight(n((K, T)) / fk[:, None], "e4m3")
    wsp = pack_weight(n((K, N)) * 1 / np.sqrt(K) * fk[:, None], "e2m1")
    return {
        "xq_words": xqp[0],
        "xq_scales": xqp[1],
        "ea": (n((K, N)) * 1 / np.sqrt(K) * fk[:, None]).astype(np.float32),
        "eb": (n((K, N)) * 1 / np.sqrt(K) * fk[:, None]).astype(np.float32),
        "sh": (np.random.uniform(0.2, 0.8, (1, N))).astype(np.float32),
        "ws_words": wsp[0],
        "ws_scales": wsp[1],
        "offs": striped(idx),
    }


def reference(xq_words, xq_scales, ea, eb, sh, ws_words, ws_scales, offs):
    idx = unstriped(offs)
    xqu = unpack_weight(xq_words, xq_scales, "e4m3")
    wsu = unpack_weight(ws_words, ws_scales, "e2m1")
    em = f64(eb) + f64(sh) * (f64(ea) - f64(eb))
    emq = mxq(em, 0, "e4m3")
    xqidxg = xqu[:, idx]
    y = emq.T @ xqidxg + wsu.T @ xqidxg
    return y

@@ -1,0 +1,231 @@
+from contextlib import ExitStack
+
+import concourse.mybir as mybir
+from concourse.masks import make_identity
+
+K, T, J, N = 1024, 2048, 512, 512
+FLOPS = 2 * 2 * K * J * N
+
+F32 = mybir.dt.float32
+BF16 = mybir.dt.bfloat16
+I32 = mybir.dt.int32
+U32 = mybir.dt.uint32
+U16 = mybir.dt.uint16
+U8 = mybir.dt.uint8
+FP8X4 = mybir.dt.float8_e4m3fn_x4
+FP4X4 = mybir.dt.float4_e2m1fn_x4
+MULT = mybir.AluOpType.mult
+ADD = mybir.AluOpType.add
+SUB = mybir.AluOpType.subtract
+COPY = mybir.ActivationFunctionType.Copy
+
+P = 128
+PACK = 4
+PASSES = K // (P * PACK)
+TILES = N // P
+
+
+def tile_list_merged_experts_kernel(tc, xq_words, xq_scales, ea, eb, sh, ws_words, ws_scales, offs, out):
+    nc = tc.nc
+    with ExitStack() as ctx:
+        keep = ctx.enter_context(tc.tile_pool(name="keep", bufs=1))
+        work = ctx.enter_context(tc.tile_pool(name="work", bufs=2))
+        psum = ctx.enter_context(tc.psum_pool(name="psum", bufs=1))
+
+        whole = {}
+
+        def load_expert(src, name, z, c0, c1):
+            t = keep.tile([P, PACK, c1 - c0], F32, name="%s_%d_%d" % (name, z, c0))
+            rows = src[512 * z : 512 * (z + 1), c0:c1]
+            nc.sync.dma_start(t[:], rows.rearrange("(p t) c -> p t c", t=PACK))
+            whole[name, z, c0] = t
+            return {m: t[:, :, m * P - c0 : (m + 1) * P - c0] for m in range(c0 // P, c1 // P)}
+
+        def load_words(z):
+            t = keep.tile([P, T], I32, name="x_table_%d" % z, align_bytes=64)
+            nc.sync.dma_start(t[:], xq_words[z].rearrange("p c r -> p (c r)").bitcast(I32))
+            return t
+
+        x_scale_table = keep.tile([P, T], U8, name="x_scale_table", align_bytes=64)
+        nc.gpsimd.memset(x_scale_table[:].bitcast(I32), 0)
+        ident = keep.tile([P, P], F32, name="ident")
+        make_identity(nc, ident[:])
+        ws_scale = keep.tile([P, PASSES, N], U8, name="ws_scale", align_bytes=64)
+        nc.vector.memset(ws_scale[:].rearrange("p z c -> p (z c)").bitcast(I32), 0)
+        x_scale_moved = keep.tile([P, J], U8, name="x_scale_moved", align_bytes=64)
+        nc.vector.memset(x_scale_moved[:].bitcast(I32), 0)
+
+        a_raw = [{}, {}]
+        b_raw = [{}, {}]
+        x_table = [None, None]
+        share = keep.tile([P, TILES], F32, name="share")
+        with nc.allow_non_contiguous_dma(reason="one share to a partition"):
+            nc.sync.dma_start(share[:], sh.rearrange("o (m n) -> n (o m)", n=P))
+        b_raw[0].update(load_expert(eb, "b", 0, 0, 256))
+        offsets = keep.tile([P, J // 16], U16, name="offsets")
+        nc.sync.dma_start(offsets[:], offs)
+        for q in range(4):
+            nc.sync.dma_start(
+                x_scale_table[32 * q : 32 * q + 8, :].bitcast(I32),
+                xq_scales[:, 4 * q : 4 * q + 4, :].bitcast(I32),
+            )
+        x_scale_both = keep.tile([P, J], U8, name="x_scale_both", align_bytes=64)
+        nc.vector.tensor_copy(x_scale_both[:], x_scale_table[:].indirect(offsets[:]))
+        a_raw[0].update(load_expert(ea, "a", 0, 0, 256))
+        x_table[0] = load_words(0)
+        for q in range(4):
+            nc.sync.dma_start(
+                ws_scale[32 * q : 32 * q + 4, :, :].bitcast(I32),
+                ws_scales[:, 4 * q : 4 * q + 4, :].rearrange("z r c -> r z c").bitcast(I32),
+            )
+        b_raw[1].update(load_expert(eb, "b", 1, 256, 512))
+        b_raw[0].update(load_expert(eb, "b", 0, 256, 512))
+        a_raw[0].update(load_expert(ea, "a", 0, 256, 512))
+        nc.sync.dma_start(x_scale_moved[0:100, :].bitcast(I32), x_scale_both[4:104, :].bitcast(I32))
+        b_raw[1].update(load_expert(eb, "b", 1, 0, 256))
+        a_raw[1].update(load_expert(ea, "a", 1, 0, 256))
+        a_raw[1].update(load_expert(ea, "a", 1, 256, 384))
+        ws_codes = keep.tile([P, PASSES, 2 * N], U8, name="ws_codes", align_bytes=64)
+        nc.sync.dma_start(ws_codes[:].bitcast(I32), ws_words.rearrange("z p c -> p z c").bitcast(I32))
+        x_table[1] = load_words(1)
+        a_raw[1].update(load_expert(ea, "a", 1, 384, 512))
+
+        rest = keep.tile([P, TILES], F32, name="rest")
+        nc.vector.tensor_scalar(rest[:], share[:], -1.0, 1.0, MULT, ADD)
+        spread = psum.tile([P, 2 * P], F32, name="spread", tag="bank7")
+        for m in (2, 3):
+            nc.tensor.transpose(
+                spread[:, (m - 2) * P : (m - 1) * P], share[:, m : m + 1].to_broadcast([P, P]), ident[:]
+            )
+        rest_row = keep.tile([P, 1, 2 * P], F32, name="rest_row")
+        nc.scalar.activation(rest_row[:, 0, :], spread[:], COPY, bias=1.0, scale=-1.0)
+        share_row = keep.tile([P, 1, 2 * P], F32, name="share_row")
+        nc.scalar.copy(share_row[:, 0, :], spread[:])
+
+        def scaled(raw, row, c0, c1, name):
+            s = keep.tile([P, PACK, c1 - c0], F32, name=name)
+            nc.vector.tensor_tensor(s[:], raw, row[:, :, c0:c1].to_broadcast([P, PACK, c1 - c0]), MULT)
+            return s
+
+        x_codes = [None, None]
+        x_scale = [x_scale_both, x_scale_moved]
+
+        def gather_words(z):
+            t = keep.tile([P, J], U32, name="x_codes_%d" % z, align_bytes=64)
+            nc.vector.tensor_copy(t[:], x_table[z][:].bitcast(U32).indirect(offsets[:]))
+            x_codes[z] = t
+
+        em_bf = {}
+        em_group = {}
+        for z, m0, m1 in ((0, 0, 2), (0, 2, 4), (1, 0, 2), (1, 2, 3), (1, 3, 4)):
+            g = keep.tile([P, (m1 - m0) * P * PACK], BF16, name="em_bf_%d_%d" % (z, m0), align_bytes=64)
+            em_group[z, m0] = g
+            for m in range(m0, m1):
+                em_bf[z, m] = g[:, (m - m0) * P * PACK : (m - m0 + 1) * P * PACK]
+        em_codes = {}
+        em_scale = {}
+
+        def by_pairs(ap):
+            return ap.rearrange("p t (c i) -> p c t i", i=2)
+
+        def woven_add(z, c0, c1, first, second):
+            g = em_bf[z, c0 // P][:, (c0 % P) * PACK : (c0 % P + c1 - c0) * PACK]
+            nc.vector.tensor_tensor(
+                g.rearrange("p (c i t) -> p c t i", i=2, t=PACK), by_pairs(first), by_pairs(second), ADD
+            )
+
+        def quantise(z, m0, m1):
+            width = (m1 - m0) * P
+            codes = keep.tile([P, width], U32, name="em_codes_%d_%d" % (z, m0), align_bytes=64)
+            scale = keep.tile([P, width], U8, name="em_scale_%d_%d" % (z, m0), align_bytes=64)
+            nc.vector.quantize_mx(
+                out=codes[:].bitcast(FP8X4), scales=scale[:], in_=em_group[z, m0][:]
+            )
+            for m in range(m0, m1):
+                em_codes[z, m] = codes[:, (m - m0) * P : (m - m0 + 1) * P]
+                em_scale[z, m] = scale[:, (m - m0) * P : (m - m0 + 1) * P]
+
+        def turned(raw, bank_no):
+            bank = psum.tile([P, 2, 2, P], F32, name="bank", tag="bank%d" % bank_no)
+            for t in range(PACK):
+                nc.tensor.transpose(bank[:, t % 2, t // 2, :], raw[:, t, :], ident[:])
+            return bank[:].rearrange("n e u p -> n (u p) e")
+
+        def merge_turned(z, m, bank_no):
+            b_t = turned(b_raw[z][m], bank_no)
+            a_t = turned(a_raw[z][m], bank_no + 1)
+            part = work.tile([P, 2 * P, 2], F32, name="part")
+            nc.scalar.activation(part[:], a_t, COPY, scale=share[:, m : m + 1])
+            mix = work.tile([P, 2 * P, 2], BF16, name="mix", align_bytes=64)
+            nc.vector.scalar_tensor_tensor(mix[:], b_t, rest[:, m : m + 1], part[:], MULT, ADD)
+            words = mix[:].rearrange("n w e -> n (w e)").bitcast(F32)
+            back = psum.tile([P, 2, P], F32, name="back", tag="bank%d" % (bank_no + 1))
+            for u in range(2):
+                nc.tensor.transpose(back[:, u, :], words[:, u * P : (u + 1) * P], ident[:])
+            g = em_bf[z, m]
+            nc.scalar.copy(g.bitcast(F32).rearrange("p (n u) -> p n u", u=2), back[:].rearrange("p u n -> p n u"))
+
+        acc = {}
+        done = [0] * TILES
+
+        def open_acc(m):
+            acc[m] = psum.tile([P, J], F32, name="acc_%d" % m, tag="bank%d" % (4 + m))
+
+        def product(m, z, codes, scale):
+            nc.tensor.matmul_mx(
+                out=acc[m][:],
+                lhsT=codes,
+                lhsT_scale=scale,
+                rhs=x_codes[z][:].bitcast(FP8X4),
+                rhs_scale=x_scale[z][:],
+                start=(done[m] == 0),
+                stop=(done[m] == 2 * PASSES - 1),
+            )
+            done[m] = done[m] + 1
+
+        def shared_product(z, m):
+            product(m, z, ws_codes[:, z, 2 * P * m : 2 * P * (m + 1)].bitcast(FP4X4), ws_scale[:, z, P * m : P * (m + 1)])
+
+        def merged_product(z, m):
+            product(m, z, em_codes[z, m].bitcast(FP8X4), em_scale[z, m])
+
+        def store(m):
+            res = keep.tile([P, J], F32, name="res_%d" % m)
+            nc.scalar.copy(res[:], acc[m][:])
+            nc.sync.dma_start(out[m * P : (m + 1) * P, :], res[:])
+
+        merge_turned(0, 0, 0)
+        merge_turned(0, 1, 2)
+        gather_words(0)
+        quantise(0, 0, 2)
+
+        b1 = scaled(whole["b", 1, 256][:], rest_row, 0, 256, "b1")
+        b02 = scaled(b_raw[0][2], rest_row, 0, 128, "b02")
+        a02 = scaled(a_raw[0][2], share_row, 0, 128, "a02")
+        merge_turned(0, 3, 4)
+        woven_add(0, 256, 384, a02[:], b02[:])
+        quantise(0, 2, 4)
+        merge_turned(1, 0, 0)
+        merge_turned(1, 1, 2)
+        a12 = scaled(a_raw[1][2], share_row, 0, 128, "a12")
+        woven_add(1, 256, 384, a12[:], b1[:, :, 0:128])
+        quantise(1, 2, 3)
+        quantise(1, 0, 2)
+        for m in range(TILES):
+            open_acc(m)
+            shared_product(0, m)
+        for m in range(TILES):
+            merged_product(0, m)
+
+        gather_words(1)
+        for m in (2, 0, 1):
+            shared_product(1, m)
+            merged_product(1, m)
+            store(m)
+        shared_product(1, 3)
+        halves = [scaled(a_raw[1][3][:, :, 64 * h : 64 * (h + 1)], share_row, 128 + 64 * h, 192 + 64 * h, "a13_%d" % h) for h in range(2)]
+        for h in range(2):
+            woven_add(1, 384 + 64 * h, 448 + 64 * h, halves[h][:], b1[:, :, 128 + 64 * h : 192 + 64 * h])
+        quantise(1, 3, 4)
+        merged_product(1, 3)
+        store(3)

@@ -29,7 +29,7 @@ def tile_list_merged_experts_kernel(tc, xq_words, xq_scales, ea, eb, sh, ws_word
     nc = tc.nc
     with ExitStack() as ctx:
         keep = ctx.enter_context(tc.tile_pool(name="keep", bufs=1))
-        work = ctx.enter_context(tc.tile_pool(name="work", bufs=2))
+        work = ctx.enter_context(tc.tile_pool(name="work", bufs=4))
         psum = ctx.enter_context(tc.psum_pool(name="psum", bufs=1))
 
         whole = {}
@@ -58,49 +58,57 @@ def tile_list_merged_experts_kernel(tc, xq_words, xq_scales, ea, eb, sh, ws_word
         a_raw = [{}, {}]
         b_raw = [{}, {}]
         x_table = [None, None]
-        share = keep.tile([P, TILES], F32, name="share")
-        with nc.allow_non_contiguous_dma(reason="one share to a partition"):
-            nc.sync.dma_start(share[:], sh.rearrange("o (m n) -> n (o m)", n=P))
-        b_raw[0].update(load_expert(eb, "b", 0, 0, 256))
+        ws_codes = [keep.tile([P, 2 * N], U8, name="ws_codes_%d" % z, align_bytes=64) for z in range(PASSES)]
+        share_quads = keep.tile([P, 4], F32, name="share_quads")
+        nc.sync.dma_start(share_quads[:], sh.rearrange("o (q j) -> q (o j)", j=4))
         offsets = keep.tile([P, J // 16], U16, name="offsets")
         nc.sync.dma_start(offsets[:], offs)
-        for q in range(4):
+        for q in (0, 2, 1, 3):
             nc.sync.dma_start(
                 x_scale_table[32 * q : 32 * q + 8, :].bitcast(I32),
                 xq_scales[:, 4 * q : 4 * q + 4, :].bitcast(I32),
             )
         x_scale_both = keep.tile([P, J], U8, name="x_scale_both", align_bytes=64)
         nc.vector.tensor_copy(x_scale_both[:], x_scale_table[:].indirect(offsets[:]))
-        a_raw[0].update(load_expert(ea, "a", 0, 0, 256))
-        x_table[0] = load_words(0)
-        for q in range(4):
+        b_raw[0].update(load_expert(eb, "b", 0, 256, 512))
+        a_raw[0].update(load_expert(ea, "a", 0, 256, 512))
+        for q in (0, 2, 1, 3):
             nc.sync.dma_start(
                 ws_scale[32 * q : 32 * q + 4, :, :].bitcast(I32),
                 ws_scales[:, 4 * q : 4 * q + 4, :].rearrange("z r c -> r z c").bitcast(I32),
             )
-        b_raw[1].update(load_expert(eb, "b", 1, 256, 512))
-        b_raw[0].update(load_expert(eb, "b", 0, 256, 512))
-        a_raw[0].update(load_expert(ea, "a", 0, 256, 512))
+        b_raw[0].update(load_expert(eb, "b", 0, 0, 256))
+        a_raw[0].update(load_expert(ea, "a", 0, 0, 256))
         nc.sync.dma_start(x_scale_moved[0:100, :].bitcast(I32), x_scale_both[4:104, :].bitcast(I32))
-        b_raw[1].update(load_expert(eb, "b", 1, 0, 256))
-        a_raw[1].update(load_expert(ea, "a", 1, 0, 256))
+        x_table[0] = load_words(0)
+        b_raw[1].update(load_expert(eb, "b", 1, 0, 512))
         a_raw[1].update(load_expert(ea, "a", 1, 256, 384))
-        ws_codes = keep.tile([P, PASSES, 2 * N], U8, name="ws_codes", align_bytes=64)
-        nc.sync.dma_start(ws_codes[:].bitcast(I32), ws_words.rearrange("z p c -> p z c").bitcast(I32))
+        a_raw[1].update(load_expert(ea, "a", 1, 0, 256))
+        nc.sync.dma_start(ws_codes[0][:].bitcast(I32), ws_words[0].bitcast(I32))
         x_table[1] = load_words(1)
+        nc.sync.dma_start(ws_codes[1][:].bitcast(I32), ws_words[1].bitcast(I32))
         a_raw[1].update(load_expert(ea, "a", 1, 384, 512))
 
-        rest = keep.tile([P, TILES], F32, name="rest")
-        nc.vector.tensor_scalar(rest[:], share[:], -1.0, 1.0, MULT, ADD)
-        spread = psum.tile([P, 2 * P], F32, name="spread", tag="bank7")
-        for m in (2, 3):
-            nc.tensor.transpose(
-                spread[:, (m - 2) * P : (m - 1) * P], share[:, m : m + 1].to_broadcast([P, P]), ident[:]
-            )
-        rest_row = keep.tile([P, 1, 2 * P], F32, name="rest_row")
-        nc.scalar.activation(rest_row[:, 0, :], spread[:], COPY, bias=1.0, scale=-1.0)
-        share_row = keep.tile([P, 1, 2 * P], F32, name="share_row")
-        nc.scalar.copy(share_row[:, 0, :], spread[:])
+        spread = psum.tile([P, 4, P], F32, name="spread", tag="bank7")
+        for j in range(4):
+            nc.tensor.transpose(spread[:, j, :], share_quads[:, j : j + 1].to_broadcast([P, P]), ident[:])
+        rest_row = keep.tile([P, 1, N], F32, name="rest_row")
+        nc.scalar.activation(
+            rest_row[:, 0, 256:512].rearrange("p (q j) -> p q j", j=4),
+            spread[:, :, 64:128].rearrange("p j q -> p q j"),
+            COPY,
+            bias=1.0,
+            scale=-1.0,
+        )
+        share_row = keep.tile([P, 1, N], F32, name="share_row")
+        nc.scalar.copy(share_row[:, 0, :].rearrange("p (q j) -> p q j", j=4), spread[:].rearrange("p j q -> p q j"))
+        upright = psum.tile([P, 2, P], F32, name="upright", tag="bank6")
+        for m in range(2):
+            nc.tensor.transpose(upright[:, m, :], share_row[:, 0, m * P : (m + 1) * P], ident[:])
+        share = keep.tile([P, 2], F32, name="share")
+        nc.scalar.copy(share[:], upright[:, :, 0])
+        rest = keep.tile([P, 2], F32, name="rest")
+        nc.scalar.activation(rest[:], upright[:, :, 0], COPY, bias=1.0, scale=-1.0)
 
         def scaled(raw, row, c0, c1, name):
             s = keep.tile([P, PACK, c1 - c0], F32, name=name)
@@ -117,10 +125,12 @@ def tile_list_merged_experts_kernel(tc, xq_words, xq_scales, ea, eb, sh, ws_word
 
         em_bf = {}
         em_group = {}
+        group_of = {}
         for z, m0, m1 in ((0, 0, 2), (0, 2, 4), (1, 0, 2), (1, 2, 3), (1, 3, 4)):
             g = keep.tile([P, (m1 - m0) * P * PACK], BF16, name="em_bf_%d_%d" % (z, m0), align_bytes=64)
             em_group[z, m0] = g
             for m in range(m0, m1):
+                group_of[z, m] = m0
                 em_bf[z, m] = g[:, (m - m0) * P * PACK : (m - m0 + 1) * P * PACK]
         em_codes = {}
         em_scale = {}
@@ -129,14 +139,15 @@ def tile_list_merged_experts_kernel(tc, xq_words, xq_scales, ea, eb, sh, ws_word
             return ap.rearrange("p t (c i) -> p c t i", i=2)
 
         def woven_add(z, c0, c1, first, second):
-            g = em_bf[z, c0 // P][:, (c0 % P) * PACK : (c0 % P + c1 - c0) * PACK]
+            g0 = group_of[z, c0 // P]
+            g = em_group[z, g0][:, (c0 - g0 * P) * PACK : (c1 - g0 * P) * PACK]
             nc.vector.tensor_tensor(
                 g.rearrange("p (c i t) -> p c t i", i=2, t=PACK), by_pairs(first), by_pairs(second), ADD
             )
 
-        def quantise(z, m0, m1):
+        def quantise(z, m0, m1, tag=None):
             width = (m1 - m0) * P
-            codes = keep.tile([P, width], U32, name="em_codes_%d_%d" % (z, m0), align_bytes=64)
+            codes = keep.tile([P, width], U32, name="em_codes_%d_%d" % (z, m0), align_bytes=64, tag=tag or "em_codes_%d_%d" % (z, m0))
             scale = keep.tile([P, width], U8, name="em_scale_%d_%d" % (z, m0), align_bytes=64)
             nc.vector.quantize_mx(
                 out=codes[:].bitcast(FP8X4), scales=scale[:], in_=em_group[z, m0][:]
@@ -145,87 +156,117 @@ def tile_list_merged_experts_kernel(tc, xq_words, xq_scales, ea, eb, sh, ws_word
                 em_codes[z, m] = codes[:, (m - m0) * P : (m - m0 + 1) * P]
                 em_scale[z, m] = scale[:, (m - m0) * P : (m - m0 + 1) * P]
 
+        mixed = {}
+
         def turned(raw, bank_no):
             bank = psum.tile([P, 2, 2, P], F32, name="bank", tag="bank%d" % bank_no)
             for t in range(PACK):
                 nc.tensor.transpose(bank[:, t % 2, t // 2, :], raw[:, t, :], ident[:])
             return bank[:].rearrange("n e u p -> n (u p) e")
 
-        def merge_turned(z, m, bank_no):
-            b_t = turned(b_raw[z][m], bank_no)
-            a_t = turned(a_raw[z][m], bank_no + 1)
+        def mix_turned(z, m, bank_b, bank_a):
+            b_t = turned(b_raw[z][m], bank_b)
+            a_t = turned(a_raw[z][m], bank_a)
             part = work.tile([P, 2 * P, 2], F32, name="part")
             nc.scalar.activation(part[:], a_t, COPY, scale=share[:, m : m + 1])
             mix = work.tile([P, 2 * P, 2], BF16, name="mix", align_bytes=64)
             nc.vector.scalar_tensor_tensor(mix[:], b_t, rest[:, m : m + 1], part[:], MULT, ADD)
-            words = mix[:].rearrange("n w e -> n (w e)").bitcast(F32)
-            back = psum.tile([P, 2, P], F32, name="back", tag="bank%d" % (bank_no + 1))
+            mixed[z, m] = mix
+
+        def turn_back(z, m, bank_no):
+            words = mixed[z, m][:].rearrange("n w e -> n (w e)").bitcast(F32)
+            back = psum.tile([P, 2, P], F32, name="back", tag="bank%d" % bank_no)
             for u in range(2):
                 nc.tensor.transpose(back[:, u, :], words[:, u * P : (u + 1) * P], ident[:])
             g = em_bf[z, m]
             nc.scalar.copy(g.bitcast(F32).rearrange("p (n u) -> p n u", u=2), back[:].rearrange("p u n -> p n u"))
 
-        acc = {}
-        done = [0] * TILES
-
-        def open_acc(m):
-            acc[m] = psum.tile([P, J], F32, name="acc_%d" % m, tag="bank%d" % (4 + m))
-
-        def product(m, z, codes, scale):
+        def product(dst, z, j0, j1, codes, scale, start, stop):
             nc.tensor.matmul_mx(
-                out=acc[m][:],
+                out=dst,
                 lhsT=codes,
                 lhsT_scale=scale,
-                rhs=x_codes[z][:].bitcast(FP8X4),
-                rhs_scale=x_scale[z][:],
-                start=(done[m] == 0),
-                stop=(done[m] == 2 * PASSES - 1),
+                rhs=x_codes[z][:, j0:j1].bitcast(FP8X4),
+                rhs_scale=x_scale[z][:, j0:j1],
+                start=start,
+                stop=stop,
             )
-            done[m] = done[m] + 1
 
-        def shared_product(z, m):
-            product(m, z, ws_codes[:, z, 2 * P * m : 2 * P * (m + 1)].bitcast(FP4X4), ws_scale[:, z, P * m : P * (m + 1)])
+        def shared_product(z, piece):
+            m, j0, j1 = piece
+            step = J if j1 - j0 == J else P
+            for j in range(j0, j1, step):
+                product(
+                    acc[piece][:, j - j0 : j - j0 + step], z, j, j + step,
+                    ws_codes[z][:, 2 * P * m : 2 * P * (m + 1)].bitcast(FP4X4),
+                    ws_scale[:, z, P * m : P * (m + 1)], z == 0 and step == J, False,
+                )
 
-        def merged_product(z, m):
-            product(m, z, em_codes[z, m].bitcast(FP8X4), em_scale[z, m])
+        def merged_product(z, piece):
+            m, j0, j1 = piece
+            product(acc[piece][:], z, j0, j1, em_codes[z, m].bitcast(FP8X4), em_scale[z, m], z == 0 and j1 - j0 < J, z == PASSES - 1)
 
-        def store(m):
-            res = keep.tile([P, J], F32, name="res_%d" % m)
-            nc.scalar.copy(res[:], acc[m][:])
-            nc.sync.dma_start(out[m * P : (m + 1) * P, :], res[:])
+        def store(piece, copy):
+            m, j0, j1 = piece
+            res = keep.tile([P, j1 - j0], F32, name="res_%d_%d" % (m, j0))
+            copy(res[:], acc[piece][:])
+            nc.sync.dma_start(out[m * P : (m + 1) * P, j0:j1], res[:])
 
-        merge_turned(0, 0, 0)
-        merge_turned(0, 1, 2)
-        gather_words(0)
-        quantise(0, 0, 2)
+        pieces = [(0, 0, J), (1, 0, J), (2, 0, J), (3, 0, J // 2), (3, J // 2, J)]
+        acc = {}
 
-        b1 = scaled(whole["b", 1, 256][:], rest_row, 0, 256, "b1")
-        b02 = scaled(b_raw[0][2], rest_row, 0, 128, "b02")
-        a02 = scaled(a_raw[0][2], share_row, 0, 128, "a02")
-        merge_turned(0, 3, 4)
-        woven_add(0, 256, 384, a02[:], b02[:])
+        def first_pass(no, bank_no):
+            piece = pieces[no]
+            acc[piece] = psum.tile([P, piece[2] - piece[1]], F32, name="acc_%d" % no, tag="bank%d" % bank_no)
+            if no < 3:
+                shared_product(0, piece)
+                merged_product(0, piece)
+            else:
+                merged_product(0, piece)
+                shared_product(0, piece)
+
+        def second_pass(no):
+            shared_product(1, pieces[no])
+            merged_product(1, pieces[no])
+            store(pieces[no], nc.scalar.copy)
+
+        b0 = scaled(whole["b", 0, 256][:], rest_row, 256, 512, "b0")
+        a0 = scaled(whole["a", 0, 256][:], share_row, 256, 512, "a0")
+        woven_add(0, 256, 512, a0[:], b0[:])
         quantise(0, 2, 4)
-        merge_turned(1, 0, 0)
-        merge_turned(1, 1, 2)
-        a12 = scaled(a_raw[1][2], share_row, 0, 128, "a12")
+        mix_turned(0, 0, 0, 1)
+        mix_turned(0, 1, 2, 3)
+        turn_back(0, 0, 1)
+        turn_back(0, 1, 3)
+        gather_words(0)
+        quantise(0, 0, 2, "x_table_0")
+        b1 = scaled(whole["b", 1, 0][:, :, 256-0:512-0], rest_row, 256, 512, "b1")
+        b13 = b1[:, :, 128:256]
+        mix_turned(1, 0, 0, 1)
+        mix_turned(1, 1, 2, 3)
+        a12 = scaled(a_raw[1][2], share_row, 256, 384, "a12")
         woven_add(1, 256, 384, a12[:], b1[:, :, 0:128])
         quantise(1, 2, 3)
-        quantise(1, 0, 2)
-        for m in range(TILES):
-            open_acc(m)
-            shared_product(0, m)
-        for m in range(TILES):
-            merged_product(0, m)
-
+        turn_back(1, 0, 1)
+        turn_back(1, 1, 3)
+        first_pass(2, 4)
+        first_pass(3, 5)
+        first_pass(4, 6)
+        first_pass(0, 0)
+        first_pass(1, 2)
         gather_words(1)
-        for m in (2, 0, 1):
-            shared_product(1, m)
-            merged_product(1, m)
-            store(m)
-        shared_product(1, 3)
-        halves = [scaled(a_raw[1][3][:, :, 64 * h : 64 * (h + 1)], share_row, 128 + 64 * h, 192 + 64 * h, "a13_%d" % h) for h in range(2)]
+        quantise(1, 0, 2, "x_table_1")
+        second_pass(2)
+        second_pass(0)
+        second_pass(1)
+        for piece in pieces[3:]:
+            shared_product(1, piece)
+
+        halves = [scaled(a_raw[1][3][:, :, 64 * h : 64 * (h + 1)], share_row, 384 + 64 * h, 448 + 64 * h, "a13_%d" % h) for h in range(2)]
         for h in range(2):
-            woven_add(1, 384 + 64 * h, 448 + 64 * h, halves[h][:], b1[:, :, 128 + 64 * h : 192 + 64 * h])
+            woven_add(1, 384 + 64 * h, 448 + 64 * h, halves[h][:], b13[:, :, 64 * h : 64 * h + 64])
         quantise(1, 3, 4)
-        merged_product(1, 3)
-        store(3)
+        for piece in pieces[3:]:
+            merged_product(1, piece)
+        store(pieces[3], nc.scalar.copy)
+        store(pieces[4], nc.vector.tensor_copy)

@@ -70,23 +70,23 @@ def tile_list_merged_experts_kernel(tc, xq_words, xq_scales, ea, eb, sh, ws_word
             )
         x_scale_both = keep.tile([P, J], U8, name="x_scale_both", align_bytes=64)
         nc.vector.tensor_copy(x_scale_both[:], x_scale_table[:].indirect(offsets[:]))
-        b_raw[0].update(load_expert(eb, "b", 0, 256, 512))
-        a_raw[0].update(load_expert(ea, "a", 0, 256, 512))
+        b_raw[0].update(load_expert(eb, "b", 0, 0, 512))
         for q in (0, 2, 1, 3):
             nc.sync.dma_start(
                 ws_scale[32 * q : 32 * q + 4, :, :].bitcast(I32),
                 ws_scales[:, 4 * q : 4 * q + 4, :].rearrange("z r c -> r z c").bitcast(I32),
             )
-        b_raw[0].update(load_expert(eb, "b", 0, 0, 256))
-        a_raw[0].update(load_expert(ea, "a", 0, 0, 256))
+        a_raw[0].update(load_expert(ea, "a", 0, 0, 512))
         nc.sync.dma_start(x_scale_moved[0:100, :].bitcast(I32), x_scale_both[4:104, :].bitcast(I32))
-        x_table[0] = load_words(0)
-        b_raw[1].update(load_expert(eb, "b", 1, 0, 512))
-        a_raw[1].update(load_expert(ea, "a", 1, 256, 384))
+        b_raw[1].update(load_expert(eb, "b", 1, 0, 256))
         a_raw[1].update(load_expert(ea, "a", 1, 0, 256))
+        x_table[0] = load_words(0)
         nc.sync.dma_start(ws_codes[0][:].bitcast(I32), ws_words[0].bitcast(I32))
+        b_raw[1].update(load_expert(eb, "b", 1, 256, 384))
+        a_raw[1].update(load_expert(ea, "a", 1, 256, 384))
         x_table[1] = load_words(1)
         nc.sync.dma_start(ws_codes[1][:].bitcast(I32), ws_words[1].bitcast(I32))
+        b_raw[1].update(load_expert(eb, "b", 1, 384, 512))
         a_raw[1].update(load_expert(ea, "a", 1, 384, 512))
 
         spread = psum.tile([P, 4, P], F32, name="spread", tag="bank7")
@@ -118,10 +118,17 @@ def tile_list_merged_experts_kernel(tc, xq_words, xq_scales, ea, eb, sh, ws_word
         x_codes = [None, None]
         x_scale = [x_scale_both, x_scale_moved]
 
-        def gather_words(z):
+        def gather_whole(z):
             t = keep.tile([P, J], U32, name="x_codes_%d" % z, align_bytes=64)
             nc.vector.tensor_copy(t[:], x_table[z][:].bitcast(U32).indirect(offsets[:]))
-            x_codes[z] = t
+            x_codes[z] = [t[:, 0 : J // 2], t[:, J // 2 : J]]
+
+        def gather_halves(z):
+            x_codes[z] = []
+            for h in range(2):
+                t = keep.tile([P, J // 2], U32, name="x_codes_%d_%d" % (z, h), align_bytes=64)
+                nc.vector.tensor_copy(t[:], x_table[z][:].bitcast(U32).indirect(offsets[:, 16 * h : 16 * (h + 1)]))
+                x_codes[z].append(t[:])
 
         em_bf = {}
         em_group = {}
@@ -181,92 +188,77 @@ def tile_list_merged_experts_kernel(tc, xq_words, xq_scales, ea, eb, sh, ws_word
             g = em_bf[z, m]
             nc.scalar.copy(g.bitcast(F32).rearrange("p (n u) -> p n u", u=2), back[:].rearrange("p u n -> p n u"))
 
-        def product(dst, z, j0, j1, codes, scale, start, stop):
+        HALF = J // 2
+        acc = {}
+
+        def product(m, h, z, j0, j1, codes, scale, start, stop):
             nc.tensor.matmul_mx(
-                out=dst,
+                out=acc[m, h][:, j0:j1],
                 lhsT=codes,
                 lhsT_scale=scale,
-                rhs=x_codes[z][:, j0:j1].bitcast(FP8X4),
-                rhs_scale=x_scale[z][:, j0:j1],
+                rhs=x_codes[z][h][:, j0:j1].bitcast(FP8X4),
+                rhs_scale=x_scale[z][:, h * HALF + j0 : h * HALF + j1],
                 start=start,
                 stop=stop,
             )
 
-        def shared_product(z, piece):
-            m, j0, j1 = piece
-            step = J if j1 - j0 == J else P
-            for j in range(j0, j1, step):
-                product(
-                    acc[piece][:, j - j0 : j - j0 + step], z, j, j + step,
-                    ws_codes[z][:, 2 * P * m : 2 * P * (m + 1)].bitcast(FP4X4),
-                    ws_scale[:, z, P * m : P * (m + 1)], z == 0 and step == J, False,
-                )
+        def shared_product(z, m, h):
+            for j in range(0, HALF, P):
+                product(m, h, z, j, j + P, ws_codes[z][:, 2 * P * m : 2 * P * (m + 1)].bitcast(FP4X4),
+                        ws_scale[:, z, P * m : P * (m + 1)], False, False)
 
-        def merged_product(z, piece):
-            m, j0, j1 = piece
-            product(acc[piece][:], z, j0, j1, em_codes[z, m].bitcast(FP8X4), em_scale[z, m], z == 0 and j1 - j0 < J, z == PASSES - 1)
+        def merged_product(z, m, h):
+            product(m, h, z, 0, HALF, em_codes[z, m].bitcast(FP8X4), em_scale[z, m], z == 0, z == PASSES - 1)
 
-        def store(piece, copy):
-            m, j0, j1 = piece
-            res = keep.tile([P, j1 - j0], F32, name="res_%d_%d" % (m, j0))
-            copy(res[:], acc[piece][:])
-            nc.sync.dma_start(out[m * P : (m + 1) * P, j0:j1], res[:])
+        def first_pass(m, h, bank_no):
+            acc[m, h] = psum.tile([P, HALF], F32, name="acc_%d_%d" % (m, h), tag="bank%d" % bank_no)
+            merged_product(0, m, h)
+            shared_product(0, m, h)
 
-        pieces = [(0, 0, J), (1, 0, J), (2, 0, J), (3, 0, J // 2), (3, J // 2, J)]
-        acc = {}
+        def store(m, h, copy):
+            res = keep.tile([P, HALF], F32, name="res_%d_%d" % (m, h))
+            copy(res[:], acc[m, h][:])
+            nc.sync.dma_start(out[m * P : (m + 1) * P, h * HALF : (h + 1) * HALF], res[:])
 
-        def first_pass(no, bank_no):
-            piece = pieces[no]
-            acc[piece] = psum.tile([P, piece[2] - piece[1]], F32, name="acc_%d" % no, tag="bank%d" % bank_no)
-            if no < 3:
-                shared_product(0, piece)
-                merged_product(0, piece)
-            else:
-                merged_product(0, piece)
-                shared_product(0, piece)
+        def second_pass(m, h):
+            shared_product(1, m, h)
+            merged_product(1, m, h)
+            store(m, h, nc.scalar.copy)
 
-        def second_pass(no):
-            shared_product(1, pieces[no])
-            merged_product(1, pieces[no])
-            store(pieces[no], nc.scalar.copy)
-
-        b0 = scaled(whole["b", 0, 256][:], rest_row, 256, 512, "b0")
-        a0 = scaled(whole["a", 0, 256][:], share_row, 256, 512, "a0")
+        b0 = scaled(whole["b", 0, 0][:, :, 256:512], rest_row, 256, 512, "b0")
+        a0 = scaled(whole["a", 0, 0][:, :, 256:512], share_row, 256, 512, "a0")
         woven_add(0, 256, 512, a0[:], b0[:])
         quantise(0, 2, 4)
         mix_turned(0, 0, 0, 1)
         mix_turned(0, 1, 2, 3)
-        turn_back(0, 0, 1)
-        turn_back(0, 1, 3)
-        gather_words(0)
-        quantise(0, 0, 2, "x_table_0")
-        b1 = scaled(whole["b", 1, 0][:, :, 256-0:512-0], rest_row, 256, 512, "b1")
-        b13 = b1[:, :, 128:256]
-        mix_turned(1, 0, 0, 1)
-        mix_turned(1, 1, 2, 3)
-        a12 = scaled(a_raw[1][2], share_row, 256, 384, "a12")
-        woven_add(1, 256, 384, a12[:], b1[:, :, 0:128])
-        quantise(1, 2, 3)
+        mix_turned(1, 0, 4, 5)
+        mix_turned(1, 1, 6, 7)
+        turn_back(0, 0, 5)
+        turn_back(0, 1, 7)
         turn_back(1, 0, 1)
         turn_back(1, 1, 3)
-        first_pass(2, 4)
-        first_pass(3, 5)
-        first_pass(4, 6)
-        first_pass(0, 0)
-        first_pass(1, 2)
-        gather_words(1)
-        quantise(1, 0, 2, "x_table_1")
-        second_pass(2)
-        second_pass(0)
-        second_pass(1)
-        for piece in pieces[3:]:
-            shared_product(1, piece)
+        quantise(0, 0, 2, None)
+        gather_whole(0)
+        quantise(1, 0, 2, "x_table_0")
+        for no, (m, h) in enumerate([(2, 0), (0, 0), (1, 0), (2, 1), (0, 1), (1, 1), (3, 0), (3, 1)]):
+            first_pass(m, h, (0, 2, 4, 6, 5, 7, 1, 3)[no])
+        b12 = scaled(b_raw[1][2], rest_row, 256, 384, "b12")
+        a12 = scaled(a_raw[1][2], share_row, 256, 384, "a12")
+        woven_add(1, 256, 384, a12[:], b12[:])
+        quantise(1, 2, 3)
 
+        gather_halves(1)
+        for h in range(2):
+            for m in (0, 1, 2):
+                second_pass(m, h)
+        for h in range(2):
+            shared_product(1, 3, h)
+        b13 = scaled(b_raw[1][3], rest_row, 384, 512, "b13")
         halves = [scaled(a_raw[1][3][:, :, 64 * h : 64 * (h + 1)], share_row, 384 + 64 * h, 448 + 64 * h, "a13_%d" % h) for h in range(2)]
         for h in range(2):
             woven_add(1, 384 + 64 * h, 448 + 64 * h, halves[h][:], b13[:, :, 64 * h : 64 * h + 64])
         quantise(1, 3, 4)
-        for piece in pieces[3:]:
-            merged_product(1, piece)
-        store(pieces[3], nc.scalar.copy)
-        store(pieces[4], nc.vector.tensor_copy)
+        for h in range(2):
+            merged_product(1, 3, h)
+        store(3, 0, nc.scalar.copy)
+        store(3, 1, nc.vector.tensor_copy)

@@ -16,248 +16,258 @@ FP8X4 = mybir.dt.float8_e4m3fn_x4
 FP4X4 = mybir.dt.float4_e2m1fn_x4
 MULT = mybir.AluOpType.mult
 ADD = mybir.AluOpType.add
-SUB = mybir.AluOpType.subtract
 COPY = mybir.ActivationFunctionType.Copy
 
 P = 128
 PACK = 4
-PASSES = K // (P * PACK)
-TILES = N // P
+K_PASS = P * PACK
+PASSES = K // K_PASS
+HALF = J // 2
+PAIR = 2 * P
+SCALE_ROWS = 4
+QUADRANTS = (0, 2, 1, 3)
+ALIGN = 64
 
 
 def tile_list_merged_experts_kernel(tc, xq_words, xq_scales, ea, eb, sh, ws_words, ws_scales, offs, out):
     nc = tc.nc
     with ExitStack() as ctx:
         keep = ctx.enter_context(tc.tile_pool(name="keep", bufs=1))
-        work = ctx.enter_context(tc.tile_pool(name="work", bufs=4))
+        turned_work = ctx.enter_context(tc.tile_pool(name="turned_work", bufs=4))
         psum = ctx.enter_context(tc.psum_pool(name="psum", bufs=1))
 
-        whole = {}
+        def bank(shape, number):
+            return psum.tile(shape, F32, name="in_bank", tag="bank%d" % number)
 
-        def load_expert(src, name, z, c0, c1):
-            t = keep.tile([P, PACK, c1 - c0], F32, name="%s_%d_%d" % (name, z, c0))
-            rows = src[512 * z : 512 * (z + 1), c0:c1]
-            nc.sync.dma_start(t[:], rows.rearrange("(p t) c -> p t c", t=PACK))
-            whole[name, z, c0] = t
-            return {m: t[:, :, m * P - c0 : (m + 1) * P - c0] for m in range(c0 // P, c1 // P)}
-
-        def load_words(z):
-            t = keep.tile([P, T], I32, name="x_table_%d" % z, align_bytes=64)
-            nc.sync.dma_start(t[:], xq_words[z].rearrange("p c r -> p (c r)").bitcast(I32))
-            return t
-
-        x_scale_table = keep.tile([P, T], U8, name="x_scale_table", align_bytes=64)
+        x_scale_table = keep.tile([P, T], U8, name="x_scale_table", align_bytes=ALIGN)
         nc.gpsimd.memset(x_scale_table[:].bitcast(I32), 0)
         ident = keep.tile([P, P], F32, name="ident")
         make_identity(nc, ident[:])
-        ws_scale = keep.tile([P, PASSES, N], U8, name="ws_scale", align_bytes=64)
+        ws_scale = keep.tile([P, PASSES, N], U8, name="ws_scale", align_bytes=ALIGN)
         nc.vector.memset(ws_scale[:].rearrange("p z c -> p (z c)").bitcast(I32), 0)
-        x_scale_moved = keep.tile([P, J], U8, name="x_scale_moved", align_bytes=64)
-        nc.vector.memset(x_scale_moved[:].bitcast(I32), 0)
+        x_scale_pass1 = keep.tile([P, J], U8, name="x_scale_pass1", align_bytes=ALIGN)
+        nc.vector.memset(x_scale_pass1[:].bitcast(I32), 0)
 
-        a_raw = [{}, {}]
-        b_raw = [{}, {}]
-        x_table = [None, None]
-        ws_codes = [keep.tile([P, 2 * N], U8, name="ws_codes_%d" % z, align_bytes=64) for z in range(PASSES)]
-        share_quads = keep.tile([P, 4], F32, name="share_quads")
-        nc.sync.dma_start(share_quads[:], sh.rearrange("o (q j) -> q (o j)", j=4))
+        def load_expert(name, src, z, c0, c1):
+            raw = keep.tile([P, PACK, c1 - c0], F32, name=name, align_bytes=ALIGN)
+            rows = src[K_PASS * z : K_PASS * (z + 1), c0:c1]
+            nc.sync.dma_start(raw[:], rows.rearrange("(p t) c -> p t c", t=PACK))
+            return raw
+
+        def load_x_words(z):
+            table = keep.tile([P, T], I32, name="x_table_%d" % z, align_bytes=ALIGN)
+            nc.sync.dma_start(table[:], xq_words[z].rearrange("p c r -> p (c r)").bitcast(I32))
+            return table
+
+        def load_ws_words(z):
+            codes = keep.tile([P, 2 * N], U8, name="ws_codes_%d" % z, align_bytes=ALIGN)
+            nc.sync.dma_start(codes[:].bitcast(I32), ws_words[z].bitcast(I32))
+            return codes
+
+        share_quads = keep.tile([P, PACK], F32, name="share_quads")
+        nc.sync.dma_start(share_quads[:], sh.rearrange("o (q j) -> q (o j)", j=PACK))
         offsets = keep.tile([P, J // 16], U16, name="offsets")
         nc.sync.dma_start(offsets[:], offs)
-        for q in (0, 2, 1, 3):
-            nc.sync.dma_start(
-                x_scale_table[32 * q : 32 * q + 8, :].bitcast(I32),
-                xq_scales[:, 4 * q : 4 * q + 4, :].bitcast(I32),
-            )
-        x_scale_both = keep.tile([P, J], U8, name="x_scale_both", align_bytes=64)
-        nc.vector.tensor_copy(x_scale_both[:], x_scale_table[:].indirect(offsets[:]))
-        b_raw[0].update(load_expert(eb, "b", 0, 0, 512))
-        for q in (0, 2, 1, 3):
-            nc.sync.dma_start(
-                ws_scale[32 * q : 32 * q + 4, :, :].bitcast(I32),
-                ws_scales[:, 4 * q : 4 * q + 4, :].rearrange("z r c -> r z c").bitcast(I32),
-            )
-        a_raw[0].update(load_expert(ea, "a", 0, 0, 512))
-        nc.sync.dma_start(x_scale_moved[0:100, :].bitcast(I32), x_scale_both[4:104, :].bitcast(I32))
-        b_raw[1].update(load_expert(eb, "b", 1, 0, 256))
-        a_raw[1].update(load_expert(ea, "a", 1, 0, 256))
-        x_table[0] = load_words(0)
-        nc.sync.dma_start(ws_codes[0][:].bitcast(I32), ws_words[0].bitcast(I32))
-        b_raw[1].update(load_expert(eb, "b", 1, 256, 384))
-        a_raw[1].update(load_expert(ea, "a", 1, 256, 384))
-        x_table[1] = load_words(1)
-        nc.sync.dma_start(ws_codes[1][:].bitcast(I32), ws_words[1].bitcast(I32))
-        b_raw[1].update(load_expert(eb, "b", 1, 384, 512))
-        a_raw[1].update(load_expert(ea, "a", 1, 384, 512))
 
-        spread = psum.tile([P, 4, P], F32, name="spread", tag="bank7")
-        for j in range(4):
+        for q in QUADRANTS:
+            nc.sync.dma_start(
+                x_scale_table[32 * q : 32 * q + PASSES * SCALE_ROWS, :].bitcast(I32),
+                xq_scales[:, SCALE_ROWS * q : SCALE_ROWS * (q + 1), :].bitcast(I32),
+            )
+        x_scale_both = keep.tile([P, J], U8, name="x_scale_both", align_bytes=ALIGN)
+        nc.vector.tensor_copy(x_scale_both[:], x_scale_table[:].indirect(offsets[:]))
+
+        eb0 = load_expert("eb0", eb, 0, 0, N)
+        ea0_direct = load_expert("ea0_direct", ea, 0, PAIR, N)
+        for q in QUADRANTS:
+            nc.sync.dma_start(
+                ws_scale[32 * q : 32 * q + SCALE_ROWS, :, :].bitcast(I32),
+                ws_scales[:, SCALE_ROWS * q : SCALE_ROWS * (q + 1), :].rearrange("z r c -> r z c").bitcast(I32),
+            )
+        ea0_turned = load_expert("ea0_turned", ea, 0, 0, PAIR)
+        live = 96 + SCALE_ROWS
+        nc.sync.dma_start(
+            x_scale_pass1[0:live, :].bitcast(I32), x_scale_both[SCALE_ROWS : SCALE_ROWS + live, :].bitcast(I32)
+        )
+        x_scale = [x_scale_both, x_scale_pass1]
+        ea1_turned = load_expert("ea1_turned", ea, 1, 0, PAIR)
+        eb1_turned = load_expert("eb1_turned", eb, 1, 0, PAIR)
+        x_table0 = load_x_words(0)
+        ws_codes = [load_ws_words(0)]
+        eb1_tile2 = load_expert("eb1_tile2", eb, 1, 2 * P, 3 * P)
+        ea1_tile2 = load_expert("ea1_tile2", ea, 1, 2 * P, 3 * P)
+        x_table1 = load_x_words(1)
+        ws_codes.append(load_ws_words(1))
+        eb1_tile3 = load_expert("eb1_tile3", eb, 1, 3 * P, N)
+        ea1_tile3 = load_expert("ea1_tile3", ea, 1, 3 * P, N)
+
+        spread = bank([P, PACK, P], 7)
+        for j in range(PACK):
             nc.tensor.transpose(spread[:, j, :], share_quads[:, j : j + 1].to_broadcast([P, P]), ident[:])
-        rest_row = keep.tile([P, 1, N], F32, name="rest_row")
+        rest_row = keep.tile([P, 1, PAIR], F32, name="rest_row")
         nc.scalar.activation(
-            rest_row[:, 0, 256:512].rearrange("p (q j) -> p q j", j=4),
-            spread[:, :, 64:128].rearrange("p j q -> p q j"),
+            rest_row[:, 0, :].rearrange("p (q j) -> p q j", j=PACK),
+            spread[:, :, PAIR // PACK :].rearrange("p j q -> p q j"),
             COPY,
             bias=1.0,
             scale=-1.0,
         )
         share_row = keep.tile([P, 1, N], F32, name="share_row")
-        nc.scalar.copy(share_row[:, 0, :].rearrange("p (q j) -> p q j", j=4), spread[:].rearrange("p j q -> p q j"))
-        upright = psum.tile([P, 2, P], F32, name="upright", tag="bank6")
+        nc.scalar.copy(share_row[:, 0, :].rearrange("p (q j) -> p q j", j=PACK), spread[:].rearrange("p j q -> p q j"))
+        upright = bank([P, 2, P], 6)
         for m in range(2):
             nc.tensor.transpose(upright[:, m, :], share_row[:, 0, m * P : (m + 1) * P], ident[:])
-        share = keep.tile([P, 2], F32, name="share")
-        nc.scalar.copy(share[:], upright[:, :, 0])
-        rest = keep.tile([P, 2], F32, name="rest")
-        nc.scalar.activation(rest[:], upright[:, :, 0], COPY, bias=1.0, scale=-1.0)
+        share_col = keep.tile([P, 2], F32, name="share_col")
+        nc.scalar.copy(share_col[:], upright[:, :, 0])
+        rest_col = keep.tile([P, 2], F32, name="rest_col")
+        nc.scalar.activation(rest_col[:], upright[:, :, 0], COPY, bias=1.0, scale=-1.0)
 
-        def scaled(raw, row, c0, c1, name):
-            s = keep.tile([P, PACK, c1 - c0], F32, name=name)
-            nc.vector.tensor_tensor(s[:], raw, row[:, :, c0:c1].to_broadcast([P, PACK, c1 - c0]), MULT)
-            return s
+        def rounded_tile(name, tiles):
+            return keep.tile([P, tiles * P * PACK], BF16, name=name, align_bytes=ALIGN)
 
-        x_codes = [None, None]
-        x_scale = [x_scale_both, x_scale_moved]
+        def times_row(name, raw, row):
+            prod = keep.tile(list(raw.shape), F32, name=name)
+            nc.vector.tensor_tensor(prod[:], raw, row.to_broadcast(list(raw.shape)), MULT)
+            return prod
 
-        def gather_whole(z):
-            t = keep.tile([P, J], U32, name="x_codes_%d" % z, align_bytes=64)
-            nc.vector.tensor_copy(t[:], x_table[z][:].bitcast(U32).indirect(offsets[:]))
-            x_codes[z] = [t[:, 0 : J // 2], t[:, J // 2 : J]]
+        def add_and_round(dst, first, second):
+            nc.vector.tensor_tensor(
+                dst.rearrange("p (c i t) -> p c t i", i=2, t=PACK),
+                first.rearrange("p t (c i) -> p c t i", i=2),
+                second.rearrange("p t (c i) -> p c t i", i=2),
+                ADD,
+            )
 
-        def gather_halves(z):
-            x_codes[z] = []
-            for h in range(2):
-                t = keep.tile([P, J // 2], U32, name="x_codes_%d_%d" % (z, h), align_bytes=64)
-                nc.vector.tensor_copy(t[:], x_table[z][:].bitcast(U32).indirect(offsets[:, 16 * h : 16 * (h + 1)]))
-                x_codes[z].append(t[:])
+        def turn(raw, bank_number):
+            turned = bank([P, 2, 2, P], bank_number)
+            for t in range(PACK):
+                nc.tensor.transpose(turned[:, t % 2, t // 2, :], raw[:, t, :], ident[:])
+            return turned[:].rearrange("n e u p -> n (u p) e")
 
-        em_bf = {}
-        em_group = {}
-        group_of = {}
-        for z, m0, m1 in ((0, 0, 2), (0, 2, 4), (1, 0, 2), (1, 2, 3), (1, 3, 4)):
-            g = keep.tile([P, (m1 - m0) * P * PACK], BF16, name="em_bf_%d_%d" % (z, m0), align_bytes=64)
-            em_group[z, m0] = g
-            for m in range(m0, m1):
-                group_of[z, m] = m0
-                em_bf[z, m] = g[:, (m - m0) * P * PACK : (m - m0 + 1) * P * PACK]
+        def merge_turned(raw_a, raw_b, m, bank_b, bank_a):
+            b_turned = turn(raw_b[:, :, m * P : (m + 1) * P], bank_b)
+            a_turned = turn(raw_a[:, :, m * P : (m + 1) * P], bank_a)
+            a_scaled = turned_work.tile([P, 2 * P, 2], F32, name="a_scaled")
+            nc.scalar.activation(a_scaled[:], a_turned, COPY, scale=share_col[:, m : m + 1])
+            merged = turned_work.tile([P, 2 * P, 2], BF16, name="merged", align_bytes=ALIGN)
+            nc.vector.scalar_tensor_tensor(merged[:], b_turned, rest_col[:, m : m + 1], a_scaled[:], MULT, ADD)
+            return merged
+
+        def turn_back(dst, merged, bank_number):
+            words = merged[:].rearrange("n w e -> n (w e)").bitcast(F32)
+            back = bank([P, 2, P], bank_number)
+            for u in range(2):
+                nc.tensor.transpose(back[:, u, :], words[:, u * P : (u + 1) * P], ident[:])
+            nc.scalar.copy(dst.bitcast(F32).rearrange("p (n u) -> p n u", u=2), back[:].rearrange("p u n -> p n u"))
+
         em_codes = {}
         em_scale = {}
 
-        def by_pairs(ap):
-            return ap.rearrange("p t (c i) -> p c t i", i=2)
+        def quantise(rounded, z, first_tile, slot):
+            width = rounded[:].shape[1] // PACK
+            codes = keep.tile([P, width], U32, name="em_codes", tag=slot, align_bytes=ALIGN)
+            scale = keep.tile([P, width], U8, name="em_scale_%d_%d" % (z, first_tile), align_bytes=ALIGN)
+            nc.vector.quantize_mx(out=codes[:].bitcast(FP8X4), scales=scale[:], in_=rounded[:])
+            for i in range(width // P):
+                em_codes[z, first_tile + i] = codes[:, i * P : (i + 1) * P]
+                em_scale[z, first_tile + i] = scale[:, i * P : (i + 1) * P]
 
-        def woven_add(z, c0, c1, first, second):
-            g0 = group_of[z, c0 // P]
-            g = em_group[z, g0][:, (c0 - g0 * P) * PACK : (c1 - g0 * P) * PACK]
-            nc.vector.tensor_tensor(
-                g.rearrange("p (c i t) -> p c t i", i=2, t=PACK), by_pairs(first), by_pairs(second), ADD
+        def gather_words(name, table, column0, columns):
+            picked = keep.tile([P, 16 * columns], U32, name=name, align_bytes=ALIGN)
+            nc.vector.tensor_copy(
+                picked[:], table[:].bitcast(U32).indirect(offsets[:, column0 : column0 + columns])
             )
+            return picked
 
-        def quantise(z, m0, m1, tag=None):
-            width = (m1 - m0) * P
-            codes = keep.tile([P, width], U32, name="em_codes_%d_%d" % (z, m0), align_bytes=64, tag=tag or "em_codes_%d_%d" % (z, m0))
-            scale = keep.tile([P, width], U8, name="em_scale_%d_%d" % (z, m0), align_bytes=64)
-            nc.vector.quantize_mx(
-                out=codes[:].bitcast(FP8X4), scales=scale[:], in_=em_group[z, m0][:]
-            )
-            for m in range(m0, m1):
-                em_codes[z, m] = codes[:, (m - m0) * P : (m - m0 + 1) * P]
-                em_scale[z, m] = scale[:, (m - m0) * P : (m - m0 + 1) * P]
-
-        mixed = {}
-
-        def turned(raw, bank_no):
-            bank = psum.tile([P, 2, 2, P], F32, name="bank", tag="bank%d" % bank_no)
-            for t in range(PACK):
-                nc.tensor.transpose(bank[:, t % 2, t // 2, :], raw[:, t, :], ident[:])
-            return bank[:].rearrange("n e u p -> n (u p) e")
-
-        def mix_turned(z, m, bank_b, bank_a):
-            b_t = turned(b_raw[z][m], bank_b)
-            a_t = turned(a_raw[z][m], bank_a)
-            part = work.tile([P, 2 * P, 2], F32, name="part")
-            nc.scalar.activation(part[:], a_t, COPY, scale=share[:, m : m + 1])
-            mix = work.tile([P, 2 * P, 2], BF16, name="mix", align_bytes=64)
-            nc.vector.scalar_tensor_tensor(mix[:], b_t, rest[:, m : m + 1], part[:], MULT, ADD)
-            mixed[z, m] = mix
-
-        def turn_back(z, m, bank_no):
-            words = mixed[z, m][:].rearrange("n w e -> n (w e)").bitcast(F32)
-            back = psum.tile([P, 2, P], F32, name="back", tag="bank%d" % bank_no)
-            for u in range(2):
-                nc.tensor.transpose(back[:, u, :], words[:, u * P : (u + 1) * P], ident[:])
-            g = em_bf[z, m]
-            nc.scalar.copy(g.bitcast(F32).rearrange("p (n u) -> p n u", u=2), back[:].rearrange("p u n -> p n u"))
-
-        HALF = J // 2
         acc = {}
+        x_codes = {}
 
-        def product(m, h, z, j0, j1, codes, scale, start, stop):
+        def merged_product(z, m, h):
             nc.tensor.matmul_mx(
-                out=acc[m, h][:, j0:j1],
-                lhsT=codes,
-                lhsT_scale=scale,
-                rhs=x_codes[z][h][:, j0:j1].bitcast(FP8X4),
-                rhs_scale=x_scale[z][:, h * HALF + j0 : h * HALF + j1],
-                start=start,
-                stop=stop,
+                out=acc[m, h][:],
+                lhsT=em_codes[z, m].bitcast(FP8X4),
+                lhsT_scale=em_scale[z, m],
+                rhs=x_codes[z, h].bitcast(FP8X4),
+                rhs_scale=x_scale[z][:, h * HALF : (h + 1) * HALF],
+                start=(z == 0),
+                stop=(z == PASSES - 1),
             )
 
         def shared_product(z, m, h):
             for j in range(0, HALF, P):
-                product(m, h, z, j, j + P, ws_codes[z][:, 2 * P * m : 2 * P * (m + 1)].bitcast(FP4X4),
-                        ws_scale[:, z, P * m : P * (m + 1)], False, False)
+                nc.tensor.matmul_mx(
+                    out=acc[m, h][:, j : j + P],
+                    lhsT=ws_codes[z][:, 2 * P * m : 2 * P * (m + 1)].bitcast(FP4X4),
+                    lhsT_scale=ws_scale[:, z, P * m : P * (m + 1)],
+                    rhs=x_codes[z, h][:, j : j + P].bitcast(FP8X4),
+                    rhs_scale=x_scale[z][:, h * HALF + j : h * HALF + j + P],
+                    start=False,
+                    stop=False,
+                )
 
-        def merged_product(z, m, h):
-            product(m, h, z, 0, HALF, em_codes[z, m].bitcast(FP8X4), em_scale[z, m], z == 0, z == PASSES - 1)
+        def store(m, h, copy):
+            result = keep.tile([P, HALF], F32, name="result_%d_%d" % (m, h))
+            copy(result[:], acc[m, h][:])
+            nc.sync.dma_start(out[m * P : (m + 1) * P, h * HALF : (h + 1) * HALF], result[:])
 
-        def first_pass(m, h, bank_no):
-            acc[m, h] = psum.tile([P, HALF], F32, name="acc_%d_%d" % (m, h), tag="bank%d" % bank_no)
+        em0_direct = rounded_tile("em0_direct", 2)
+        b_part = times_row("b0_part", eb0[:, :, PAIR:], rest_row[:])
+        a_part = times_row("a0_part", ea0_direct[:], share_row[:, :, PAIR:])
+        add_and_round(em0_direct[:], a_part[:], b_part[:])
+        quantise(em0_direct, 0, 2, "em0_direct_codes")
+
+        merged = {}
+        for z, (raw_a, raw_b) in enumerate([(ea0_turned, eb0), (ea1_turned, eb1_turned)]):
+            for m in range(2):
+                merged[z, m] = merge_turned(raw_a, raw_b, m, 4 * z + 2 * m, 4 * z + 2 * m + 1)
+        em_turned = [rounded_tile("em%d_turned" % z, 2) for z in range(PASSES)]
+        for z in range(PASSES):
+            for m in range(2):
+                turn_back(em_turned[z][:, m * K_PASS : (m + 1) * K_PASS], merged[z, m], 4 + 2 * m + z)
+
+        picked = gather_words("x_codes_0", x_table0, 0, J // 16)
+        for h in range(2):
+            x_codes[0, h] = picked[:, h * HALF : (h + 1) * HALF]
+        em1_tile2 = rounded_tile("em1_tile2", 1)
+        b_part = times_row("b1_part_2", eb1_tile2[:], rest_row[:, :, 0:P])
+        a_part = times_row("a1_part_2", ea1_tile2[:], share_row[:, :, 2 * P : 3 * P])
+        quantise(em_turned[0], 0, 0, "eb1_tile2")
+        add_and_round(em1_tile2[:], a_part[:], b_part[:])
+        quantise(em_turned[1], 1, 0, "ea1_tile2")
+        quantise(em1_tile2, 1, 2, "em1_tile2_codes")
+
+        order = [(m, h) for m in (2, 3) for h in range(2)] + [(m, h) for h in range(2) for m in (0, 1)]
+        for number, (m, h) in enumerate(order):
+            acc[m, h] = bank([P, HALF], number)
             merged_product(0, m, h)
             shared_product(0, m, h)
 
-        def store(m, h, copy):
-            res = keep.tile([P, HALF], F32, name="res_%d_%d" % (m, h))
-            copy(res[:], acc[m, h][:])
-            nc.sync.dma_start(out[m * P : (m + 1) * P, h * HALF : (h + 1) * HALF], res[:])
-
-        def second_pass(m, h):
-            shared_product(1, m, h)
-            merged_product(1, m, h)
-            store(m, h, nc.scalar.copy)
-
-        b0 = scaled(whole["b", 0, 0][:, :, 256:512], rest_row, 256, 512, "b0")
-        a0 = scaled(whole["a", 0, 0][:, :, 256:512], share_row, 256, 512, "a0")
-        woven_add(0, 256, 512, a0[:], b0[:])
-        quantise(0, 2, 4)
-        mix_turned(0, 0, 0, 1)
-        mix_turned(0, 1, 2, 3)
-        mix_turned(1, 0, 4, 5)
-        mix_turned(1, 1, 6, 7)
-        turn_back(0, 0, 5)
-        turn_back(0, 1, 7)
-        turn_back(1, 0, 1)
-        turn_back(1, 1, 3)
-        quantise(0, 0, 2, None)
-        gather_whole(0)
-        quantise(1, 0, 2, "x_table_0")
-        for no, (m, h) in enumerate([(2, 0), (0, 0), (1, 0), (2, 1), (0, 1), (1, 1), (3, 0), (3, 1)]):
-            first_pass(m, h, (0, 2, 4, 6, 5, 7, 1, 3)[no])
-        b12 = scaled(b_raw[1][2], rest_row, 256, 384, "b12")
-        a12 = scaled(a_raw[1][2], share_row, 256, 384, "a12")
-        woven_add(1, 256, 384, a12[:], b12[:])
-        quantise(1, 2, 3)
-
-        gather_halves(1)
         for h in range(2):
-            for m in (0, 1, 2):
-                second_pass(m, h)
+            x_codes[1, h] = gather_words("x_codes_1_%d" % h, x_table1, h * HALF // 16, HALF // 16)[:]
+        for h in range(2):
+            for m in range(3):
+                shared_product(1, m, h)
+                merged_product(1, m, h)
+                store(m, h, nc.scalar.copy)
         for h in range(2):
             shared_product(1, 3, h)
-        b13 = scaled(b_raw[1][3], rest_row, 384, 512, "b13")
-        halves = [scaled(a_raw[1][3][:, :, 64 * h : 64 * (h + 1)], share_row, 384 + 64 * h, 448 + 64 * h, "a13_%d" % h) for h in range(2)]
-        for h in range(2):
-            woven_add(1, 384 + 64 * h, 448 + 64 * h, halves[h][:], b13[:, :, 64 * h : 64 * h + 64])
-        quantise(1, 3, 4)
+
+        em1_tile3 = rounded_tile("em1_tile3", 1)
+        b_part = times_row("b1_part_3", eb1_tile3[:], rest_row[:, :, P:])
+        run = P // 2
+        a_parts = [
+            times_row(
+                "a1_part_3_%d" % r,
+                ea1_tile3[:, :, r * run : (r + 1) * run],
+                share_row[:, :, 3 * P + r * run : 3 * P + (r + 1) * run],
+            )
+            for r in range(2)
+        ]
+        for r in range(2):
+            add_and_round(
+                em1_tile3[:, r * run * PACK : (r + 1) * run * PACK], a_parts[r][:], b_part[:, :, r * run : (r + 1) * run]
+            )
+        quantise(em1_tile3, 1, 3, "em1_tile3_codes")
         for h in range(2):
             merged_product(1, 3, h)
         store(3, 0, nc.scalar.copy)

from contextlib import ExitStack

import concourse.mybir as mybir
from concourse.masks import make_identity

K, T, J, N = 1024, 2048, 512, 512
FLOPS = 2 * 2 * K * J * N

F32 = mybir.dt.float32
BF16 = mybir.dt.bfloat16
I32 = mybir.dt.int32
U32 = mybir.dt.uint32
U16 = mybir.dt.uint16
U8 = mybir.dt.uint8
FP8X4 = mybir.dt.float8_e4m3fn_x4
FP4X4 = mybir.dt.float4_e2m1fn_x4
MULT = mybir.AluOpType.mult
ADD = mybir.AluOpType.add
COPY = mybir.ActivationFunctionType.Copy

P = 128
PACK = 4
K_PASS = P * PACK
PASSES = K // K_PASS
HALF = J // 2
PAIR = 2 * P
SCALE_ROWS = 4
QUADRANTS = (0, 2, 1, 3)
ALIGN = 64


def tile_list_merged_experts_kernel(tc, xq_words, xq_scales, ea, eb, sh, ws_words, ws_scales, offs, out):
    nc = tc.nc
    with ExitStack() as ctx:
        keep = ctx.enter_context(tc.tile_pool(name="keep", bufs=1))
        turned_work = ctx.enter_context(tc.tile_pool(name="turned_work", bufs=4))
        psum = ctx.enter_context(tc.psum_pool(name="psum", bufs=1))

        def bank(shape, number):
            return psum.tile(shape, F32, name="in_bank", tag="bank%d" % number)

        x_scale_table = keep.tile([P, T], U8, name="x_scale_table", align_bytes=ALIGN)
        nc.gpsimd.memset(x_scale_table[:].bitcast(I32), 0)
        ident = keep.tile([P, P], F32, name="ident")
        make_identity(nc, ident[:])
        ws_scale = keep.tile([P, PASSES, N], U8, name="ws_scale", align_bytes=ALIGN)
        nc.vector.memset(ws_scale[:].rearrange("p z c -> p (z c)").bitcast(I32), 0)
        x_scale_pass1 = keep.tile([P, J], U8, name="x_scale_pass1", align_bytes=ALIGN)
        nc.vector.memset(x_scale_pass1[:].bitcast(I32), 0)

        def load_expert(name, src, z, c0, c1):
            raw = keep.tile([P, PACK, c1 - c0], F32, name=name, align_bytes=ALIGN)
            rows = src[K_PASS * z : K_PASS * (z + 1), c0:c1]
            nc.sync.dma_start(raw[:], rows.rearrange("(p t) c -> p t c", t=PACK))
            return raw

        def load_x_words(z):
            table = keep.tile([P, T], I32, name="x_table_%d" % z, align_bytes=ALIGN)
            nc.sync.dma_start(table[:], xq_words[z].rearrange("p c r -> p (c r)").bitcast(I32))
            return table

        def load_ws_words(z):
            codes = keep.tile([P, 2 * N], U8, name="ws_codes_%d" % z, align_bytes=ALIGN)
            nc.sync.dma_start(codes[:].bitcast(I32), ws_words[z].bitcast(I32))
            return codes

        share_quads = keep.tile([P, PACK], F32, name="share_quads")
        nc.sync.dma_start(share_quads[:], sh.rearrange("o (q j) -> q (o j)", j=PACK))
        offsets = keep.tile([P, J // 16], U16, name="offsets")
        nc.sync.dma_start(offsets[:], offs)

        for q in QUADRANTS:
            nc.sync.dma_start(
                x_scale_table[32 * q : 32 * q + PASSES * SCALE_ROWS, :].bitcast(I32),
                xq_scales[:, SCALE_ROWS * q : SCALE_ROWS * (q + 1), :].bitcast(I32),
            )
        x_scale_both = keep.tile([P, J], U8, name="x_scale_both", align_bytes=ALIGN)
        nc.vector.tensor_copy(x_scale_both[:], x_scale_table[:].indirect(offsets[:]))

        eb0 = load_expert("eb0", eb, 0, 0, N)
        ea0_direct = load_expert("ea0_direct", ea, 0, PAIR, N)
        for q in QUADRANTS:
            nc.sync.dma_start(
                ws_scale[32 * q : 32 * q + SCALE_ROWS, :, :].bitcast(I32),
                ws_scales[:, SCALE_ROWS * q : SCALE_ROWS * (q + 1), :].rearrange("z r c -> r z c").bitcast(I32),
            )
        ea0_turned = load_expert("ea0_turned", ea, 0, 0, PAIR)
        live = 96 + SCALE_ROWS
        nc.sync.dma_start(
            x_scale_pass1[0:live, :].bitcast(I32), x_scale_both[SCALE_ROWS : SCALE_ROWS + live, :].bitcast(I32)
        )
        x_scale = [x_scale_both, x_scale_pass1]
        ea1_turned = load_expert("ea1_turned", ea, 1, 0, PAIR)
        eb1_turned = load_expert("eb1_turned", eb, 1, 0, PAIR)
        x_table0 = load_x_words(0)
        ws_codes = [load_ws_words(0)]
        eb1_tile2 = load_expert("eb1_tile2", eb, 1, 2 * P, 3 * P)
        ea1_tile2 = load_expert("ea1_tile2", ea, 1, 2 * P, 3 * P)
        x_table1 = load_x_words(1)
        ws_codes.append(load_ws_words(1))
        eb1_tile3 = load_expert("eb1_tile3", eb, 1, 3 * P, N)
        ea1_tile3 = load_expert("ea1_tile3", ea, 1, 3 * P, N)

        spread = bank([P, PACK, P], 7)
        for j in range(PACK):
            nc.tensor.transpose(spread[:, j, :], share_quads[:, j : j + 1].to_broadcast([P, P]), ident[:])
        rest_row = keep.tile([P, 1, PAIR], F32, name="rest_row")
        nc.scalar.activation(
            rest_row[:, 0, :].rearrange("p (q j) -> p q j", j=PACK),
            spread[:, :, PAIR // PACK :].rearrange("p j q -> p q j"),
            COPY,
            bias=1.0,
            scale=-1.0,
        )
        share_row = keep.tile([P, 1, N], F32, name="share_row")
        nc.scalar.copy(share_row[:, 0, :].rearrange("p (q j) -> p q j", j=PACK), spread[:].rearrange("p j q -> p q j"))
        upright = bank([P, 2, P], 6)
        for m in range(2):
            nc.tensor.transpose(upright[:, m, :], share_row[:, 0, m * P : (m + 1) * P], ident[:])
        share_col = keep.tile([P, 2], F32, name="share_col")
        nc.scalar.copy(share_col[:], upright[:, :, 0])
        rest_col = keep.tile([P, 2], F32, name="rest_col")
        nc.scalar.activation(rest_col[:], upright[:, :, 0], COPY, bias=1.0, scale=-1.0)

        def rounded_tile(name, tiles):
            return keep.tile([P, tiles * P * PACK], BF16, name=name, align_bytes=ALIGN)

        def times_row(name, raw, row):
            prod = keep.tile(list(raw.shape), F32, name=name)
            nc.vector.tensor_tensor(prod[:], raw, row.to_broadcast(list(raw.shape)), MULT)
            return prod

        def add_and_round(dst, first, second):
            nc.vector.tensor_tensor(
                dst.rearrange("p (c i t) -> p c t i", i=2, t=PACK),
                first.rearrange("p t (c i) -> p c t i", i=2),
                second.rearrange("p t (c i) -> p c t i", i=2),
                ADD,
            )

        def turn(raw, bank_number):
            turned = bank([P, 2, 2, P], bank_number)
            for t in range(PACK):
                nc.tensor.transpose(turned[:, t % 2, t // 2, :], raw[:, t, :], ident[:])
            return turned[:].rearrange("n e u p -> n (u p) e")

        def merge_turned(raw_a, raw_b, m, bank_b, bank_a):
            b_turned = turn(raw_b[:, :, m * P : (m + 1) * P], bank_b)
            a_turned = turn(raw_a[:, :, m * P : (m + 1) * P], bank_a)
            a_scaled = turned_work.tile([P, 2 * P, 2], F32, name="a_scaled")
            nc.scalar.activation(a_scaled[:], a_turned, COPY, scale=share_col[:, m : m + 1])
            merged = turned_work.tile([P, 2 * P, 2], BF16, name="merged", align_bytes=ALIGN)
            nc.vector.scalar_tensor_tensor(merged[:], b_turned, rest_col[:, m : m + 1], a_scaled[:], MULT, ADD)
            return merged

        def turn_back(dst, merged, bank_number):
            words = merged[:].rearrange("n w e -> n (w e)").bitcast(F32)
            back = bank([P, 2, P], bank_number)
            for u in range(2):
                nc.tensor.transpose(back[:, u, :], words[:, u * P : (u + 1) * P], ident[:])
            nc.scalar.copy(dst.bitcast(F32).rearrange("p (n u) -> p n u", u=2), back[:].rearrange("p u n -> p n u"))

        em_codes = {}
        em_scale = {}

        def quantise(rounded, z, first_tile, slot):
            width = rounded[:].shape[1] // PACK
            codes = keep.tile([P, width], U32, name="em_codes", tag=slot, align_bytes=ALIGN)
            scale = keep.tile([P, width], U8, name="em_scale_%d_%d" % (z, first_tile), align_bytes=ALIGN)
            nc.vector.quantize_mx(out=codes[:].bitcast(FP8X4), scales=scale[:], in_=rounded[:])
            for i in range(width // P):
                em_codes[z, first_tile + i] = codes[:, i * P : (i + 1) * P]
                em_scale[z, first_tile + i] = scale[:, i * P : (i + 1) * P]

        def gather_words(name, table, column0, columns):
            picked = keep.tile([P, 16 * columns], U32, name=name, align_bytes=ALIGN)
            nc.vector.tensor_copy(
                picked[:], table[:].bitcast(U32).indirect(offsets[:, column0 : column0 + columns])
            )
            return picked

        acc = {}
        x_codes = {}

        def merged_product(z, m, h):
            nc.tensor.matmul_mx(
                out=acc[m, h][:],
                lhsT=em_codes[z, m].bitcast(FP8X4),
                lhsT_scale=em_scale[z, m],
                rhs=x_codes[z, h].bitcast(FP8X4),
                rhs_scale=x_scale[z][:, h * HALF : (h + 1) * HALF],
                start=(z == 0),
                stop=(z == PASSES - 1),
            )

        def shared_product(z, m, h):
            for j in range(0, HALF, P):
                nc.tensor.matmul_mx(
                    out=acc[m, h][:, j : j + P],
                    lhsT=ws_codes[z][:, 2 * P * m : 2 * P * (m + 1)].bitcast(FP4X4),
                    lhsT_scale=ws_scale[:, z, P * m : P * (m + 1)],
                    rhs=x_codes[z, h][:, j : j + P].bitcast(FP8X4),
                    rhs_scale=x_scale[z][:, h * HALF + j : h * HALF + j + P],
                    start=False,
                    stop=False,
                )

        def store(m, h, copy):
            result = keep.tile([P, HALF], F32, name="result_%d_%d" % (m, h))
            copy(result[:], acc[m, h][:])
            nc.sync.dma_start(out[m * P : (m + 1) * P, h * HALF : (h + 1) * HALF], result[:])

        em0_direct = rounded_tile("em0_direct", 2)
        b_part = times_row("b0_part", eb0[:, :, PAIR:], rest_row[:])
        a_part = times_row("a0_part", ea0_direct[:], share_row[:, :, PAIR:])
        add_and_round(em0_direct[:], a_part[:], b_part[:])
        quantise(em0_direct, 0, 2, "em0_direct_codes")

        merged = {}
        for z, (raw_a, raw_b) in enumerate([(ea0_turned, eb0), (ea1_turned, eb1_turned)]):
            for m in range(2):
                merged[z, m] = merge_turned(raw_a, raw_b, m, 4 * z + 2 * m, 4 * z + 2 * m + 1)
        em_turned = [rounded_tile("em%d_turned" % z, 2) for z in range(PASSES)]
        for z in range(PASSES):
            for m in range(2):
                turn_back(em_turned[z][:, m * K_PASS : (m + 1) * K_PASS], merged[z, m], 4 + 2 * m + z)

        picked = gather_words("x_codes_0", x_table0, 0, J // 16)
        for h in range(2):
            x_codes[0, h] = picked[:, h * HALF : (h + 1) * HALF]
        em1_tile2 = rounded_tile("em1_tile2", 1)
        b_part = times_row("b1_part_2", eb1_tile2[:], rest_row[:, :, 0:P])
        a_part = times_row("a1_part_2", ea1_tile2[:], share_row[:, :, 2 * P : 3 * P])
        quantise(em_turned[0], 0, 0, "eb1_tile2")
        add_and_round(em1_tile2[:], a_part[:], b_part[:])
        quantise(em_turned[1], 1, 0, "ea1_tile2")
        quantise(em1_tile2, 1, 2, "em1_tile2_codes")

        order = [(m, h) for m in (2, 3) for h in range(2)] + [(m, h) for h in range(2) for m in (0, 1)]
        for number, (m, h) in enumerate(order):
            acc[m, h] = bank([P, HALF], number)
            merged_product(0, m, h)
            shared_product(0, m, h)

        for h in range(2):
            x_codes[1, h] = gather_words("x_codes_1_%d" % h, x_table1, h * HALF // 16, HALF // 16)[:]
        for h in range(2):
            for m in range(3):
                shared_product(1, m, h)
                merged_product(1, m, h)
                store(m, h, nc.scalar.copy)
        for h in range(2):
            shared_product(1, 3, h)

        em1_tile3 = rounded_tile("em1_tile3", 1)
        b_part = times_row("b1_part_3", eb1_tile3[:], rest_row[:, :, P:])
        run = P // 2
        a_parts = [
            times_row(
                "a1_part_3_%d" % r,
                ea1_tile3[:, :, r * run : (r + 1) * run],
                share_row[:, :, 3 * P + r * run : 3 * P + (r + 1) * run],
            )
            for r in range(2)
        ]
        for r in range(2):
            add_and_round(
                em1_tile3[:, r * run * PACK : (r + 1) * run * PACK], a_parts[r][:], b_part[:, :, r * run : (r + 1) * run]
            )
        quantise(em1_tile3, 1, 3, "em1_tile3_codes")
        for h in range(2):
            merged_product(1, 3, h)
        store(3, 0, nc.scalar.copy)
        store(3, 1, nc.vector.tensor_copy)
